import numpy as np, ml_dtypes
CORES = [23,119,17,113]
N = 4
import mx_ref
NC = 128
BF = ml_dtypes.bfloat16
def cut(t, i, w=512):
    return t[:, w * i:w * i + w]
def term(a, B):
    return np.stack([np.maximum(mx_ref.matmul(mx_ref.quantize(cut(a, i)), B), 0) for i in range(4)], axis=2).reshape(128, -1)
def setup_inputs(rng):
    def f(*shape):
        return mx_ref.flush((rng.standard_normal(shape, dtype=np.float32) * np.exp2(rng.integers(-2, 3, shape[:-1] + (1,)))).astype(BF))
    return {"a": f(N, 128, 4 * 512), "b": f(N, 128, 4 * NC)}
def setup_inputs_blocks(rng):
    d = setup_inputs(rng)
    for k in ("a", "b"): d[k] = mx_ref.spread(d[k], rng, 2)
    return d
def setup_inputs_wide(rng):
    d = setup_inputs(rng)
    for k in ("a", "b"): d[k] = mx_ref.flush((d[k].astype(np.float32) * np.exp2(rng.integers(-4, 5, (N, 1, 1))).astype(np.float32)).astype(BF))
    return d
def setup_inputs_lossless(rng):
    a = np.zeros((N, 128, 4 * 128, 4), np.float32)
    for r in range(N):
        k = rng.integers(0, 512, size=4 * 128)
        a[r, k // 4, np.arange(4 * 128), k % 4] = 1.0
    size = np.repeat(2.0 ** rng.integers(-4, 5, size=(1, 1, (4 * NC) // 4)), 4, axis=2)
    b = (rng.random((N, 128, 4 * NC)) < 0.8) * size
    return {"a": a.reshape(N, 128, 4 * 512).astype(BF), "b": b.astype(np.float32).astype(BF)}
def reference(a, b):
    Bq = [mx_ref.quantize(b[c]) for c in range(N)]
    y = np.zeros((N, 128, 4 * NC), np.float32)
    for c in range(N):
        y[c] = mx_ref.total([term(a[r], Bq[c]) for r in range(N)])
    return {"y": y}

@@ -1,0 +1,129 @@
+from concourse.bass import DstId, RemoteDMATransfer
+from concourse.mybir import dt, AluOpType, ActivationFunctionType
+
+BF, F32, MX, U8 = "bfloat16", "float32", "float8_e4m3fn_x4", "uint8"
+SCRATCH = {
+    "b_in": ("sbuf", [128, 512], BF), "a_in": ("sbuf", [128, 2048], BF),
+    "bq": ("sbuf", [128, 128], MX), "bs": ("sbuf", [128, 128], U8),
+    "aq": ("sbuf", [128, 512], MX), "asc": ("sbuf", [128, 512], U8),
+    "bxq": ("sbuf", [128, 128], MX), "bxs": ("sbuf", [128, 128], U8),
+    "apq": ("sbuf", [128, 512], MX), "aps": ("sbuf", [128, 512], U8),
+    "z": ("sbuf", [128, 516], BF),
+    "eq": ("sbuf", [128, 512], MX), "es": ("sbuf", [128, 512], U8),
+    "s": ("sbuf", [128, 512], BF), "sq": ("sbuf", [128, 128], MX), "ss": ("sbuf", [128, 128], U8),
+    "sxq": ("sbuf", [128, 128], MX), "sxs": ("sbuf", [128, 128], U8),
+    "accs": ("sbuf", [128, 512], F32), "tmp3": ("sbuf", [128, 512], F32),
+    "acc": ("sbuf", [128, 512], F32), "tmp4": ("sbuf", [128, 512], F32), "yb": ("sbuf", [128, 512], F32),
+    "ps": ("psum", [128, 4096], F32),
+}
+SEMAPHORES = (["lb", "la0", "la1", "zset", "zsel", "qe", "qb", "qa0", "qa1", "bx", "ap", "sx", "sent", "sadd", "qs",
+               "yd", "st"]
+              + ["%s_%d" % (k, i) for k in ("p1", "p2", "p3", "p4", "p5", "r1", "r2", "r3", "r4", "a4") for i in range(4)])
+
+
+def rank_program(g, core, T, topo):
+    rank = T.rank_of(core)
+    if rank is None:
+        return
+    partner = [c for c in T.cores if c != core and topo.chip(c) == topo.chip(core)][0]
+    far = [c for c in T.cores if topo.chip(c) != topo.chip(core) and topo.die(c) == topo.die(core)][0]
+    m_near, m_far = topo.mask(core, partner), topo.mask(core, far)
+    m_rest = m_near & ~m_far
+    count = lambda m: bin(m).count("1")
+    S = T.sem
+    relu = ActivationFunctionType.Relu
+    bank = lambda k: T.ps[:, 512 * k:512 * k + 128]
+    tile = lambda t, i: t[:, 128 * i:128 * i + 128]
+    codes = lambda v: v.bitcast(dt.uint8)
+    sent = [0]
+
+    def send(dst, m, out, in_, sem):
+        rid, pid, _ = topo.addr(dst)
+        g.remote_dma(out, in_, sem, S.sent, pid, rid, m)
+        sent[0] += count(m)
+
+    def part(dst, m, out, in_, sem):
+        rid, pid, _ = topo.addr(dst)
+        sent[0] += count(m)
+        return RemoteDMATransfer(dst_ids=[DstId(rid=rid, pnc=pid)], dma_engine_mask=m, remote_sem=sem, src=in_, dst=out)
+
+    g.sync.dma_start(T.b_in[:], T.b[:]).then_inc(S.lb, 16)
+    g.scalar.dma_start(T.a_in[:, 0:1024], T.a[:, 0:1024]).then_inc(S.la0, 16)
+    g.sync.dma_start(T.a_in[:, 1024:2048], T.a[:, 1024:2048]).then_inc(S.la1, 16)
+
+    v = g.vector
+    v.memset(T.z[:], 1.0).then_inc(S.zset, 1)
+    v.wait_ge(S.zsel, 1)
+    for i in range(4):
+        v.quantize_mx(tile(T.eq, i), tile(T.es, i), T.z[:, 3 - i:515 - i]).then_inc(S.qe, 1)
+    v.wait_ge(S.lb, 16)
+    v.quantize_mx(T.bq[:], T.bs[:], T.b_in[:]).then_inc(S.qb, 1)
+    for h in range(2):
+        v.wait_ge(S["la%d" % h], 16)
+        for i in (2 * h, 2 * h + 1):
+            v.quantize_mx(tile(T.aq, i), tile(T.asc, i), T.a_in[:, 512 * i:512 * i + 512]).then_inc(S["qa%d" % h], 1)
+    for i in range(4):
+        v.wait_ge(S["r2_%d" % i], 1)
+        v.wait_ge(S["r3_%d" % i], 1)
+        v.tensor_tensor(T.s[:, i:512:4], tile(T.tmp3, i), tile(T.accs, i), AluOpType.add).then_inc(S.sadd, 1)
+    v.wait_ge(S.sadd, 4)
+    v.quantize_mx(T.sq[:], T.ss[:], T.s[:]).then_inc(S.qs, 1)
+    for i in range(4):
+        v.wait_ge(S["r1_%d" % i], 1)
+        v.wait_ge(S["r4_%d" % i], 1)
+        v.tensor_tensor(T.acc[:, i:512:4], T.acc[:, i:512:4], tile(T.tmp4, i), AluOpType.add).then_inc(S["a4_%d" % i], 1)
+    for i in range(4):
+        v.wait_ge(S["a4_%d" % i], 1)
+        v.wait_ge(S["p5_%d" % i], 1)
+        v.tensor_tensor(T.yb[:, i:512:4], bank(i), T.acc[:, i:512:4], AluOpType.add).then_inc(S.yd, 1)
+
+    g.wait_ge(S.zset, 1)
+    g.affine_select(T.z[:], T.z[:], [[-1, 516]], AluOpType.is_equal, 0.0, 3, 4).then_inc(S.zsel, 1)
+    g.wait_ge(S.qb, 1)
+    send(far, m_far, T.bxs[:], T.bs[:], S.bx)
+    g.wait_ge(S.qa0, 2)
+    g.wait_ge(S.qa1, 2)
+    g.remote_dma_fused([part(far, m_far, codes(T.bxq[:]), codes(T.bq[:]), S.bx),
+                        part(partner, m_rest, T.aps[:], T.asc[:], S.ap)], local_sem=S.sent)
+    send(partner, m_near, codes(T.apq[:]), codes(T.aq[:]), S.ap)
+    g.wait_ge(S.qs, 1)
+    send(far, m_far, codes(T.sxq[:]), codes(T.sq[:]), S.sx)
+    send(far, m_far, T.sxs[:], T.ss[:], S.sx)
+    g.wait_ge(S.sent, sent[0])
+
+    t = g.tensor
+
+    def mm(k, w, ws, i, x, xs, sem):
+        t.matmul_mx(bank(k), tile(w, i), tile(ws, i), x[:], xs[:], True, True).then_inc(S["%s_%d" % (sem, i)], 1)
+
+    t.wait_ge(S.qb, 1)
+    for i in range(4):
+        if i % 2 == 0:
+            t.wait_ge(S["qa%d" % (i // 2)], 2)
+        mm(i, T.aq, T.asc, i, T.bq, T.bs, "p1")
+    t.wait_ge(S.bx, 2 * count(m_far))
+    for i in range(4):
+        mm(4 + i, T.aq, T.asc, i, T.bxq, T.bxs, "p2")
+    t.wait_ge(S.ap, count(m_rest) + count(m_near))
+    for i in range(4):
+        t.wait_ge(S["r1_%d" % i], 1)
+        mm(i, T.apq, T.aps, i, T.bxq, T.bxs, "p3")
+    for i in range(4):
+        t.wait_ge(S["r2_%d" % i], 1)
+        mm(4 + i, T.apq, T.aps, i, T.bq, T.bs, "p4")
+    t.wait_ge(S.qe, 4)
+    t.wait_ge(S.sx, 2 * count(m_far))
+    for i in range(4):
+        t.wait_ge(S["r3_%d" % i], 1)
+        mm(i, T.eq, T.es, i, T.sxq, T.sxs, "p5")
+
+    a = g.scalar
+    for k, dst in ((1, lambda i: T.acc[:, i:512:4]), (2, lambda i: tile(T.accs, i)),
+                   (3, lambda i: tile(T.tmp3, i)), (4, lambda i: tile(T.tmp4, i))):
+        for i in range(4):
+            a.wait_ge(S["p%d_%d" % (k, i)], 1)
+            a.activation(dst(i), bank(i if k % 2 else 4 + i), relu).then_inc(S["r%d_%d" % (k, i)], 1)
+
+    g.sync.wait_ge(S.yd, 4)
+    g.sync.dma_start(T.y[:], T.yb[:]).then_inc(S.st, 16)
+    g.sync.wait_ge(S.st, 16)

@@ -8,6 +8,7 @@ SCRATCH = {
     "aq": ("sbuf", [128, 512], MX), "asc": ("sbuf", [128, 512], U8),
     "bxq": ("sbuf", [128, 128], MX), "bxs": ("sbuf", [128, 128], U8),
     "apq": ("sbuf", [128, 512], MX), "aps": ("sbuf", [128, 512], U8),
+    "one": ("sbuf", [128, 516], BF), "ramp": ("sbuf", [128, 516], F32), "col": ("sbuf", [128, 1], F32),
     "z": ("sbuf", [128, 516], BF),
     "eq": ("sbuf", [128, 512], MX), "es": ("sbuf", [128, 512], U8),
     "s": ("sbuf", [128, 512], BF), "sq": ("sbuf", [128, 128], MX), "ss": ("sbuf", [128, 128], U8),
@@ -16,8 +17,8 @@ SCRATCH = {
     "acc": ("sbuf", [128, 512], F32), "tmp4": ("sbuf", [128, 512], F32), "yb": ("sbuf", [128, 512], F32),
     "ps": ("psum", [128, 4096], F32),
 }
-SEMAPHORES = (["lb", "la0", "la1", "zset", "zsel", "qe", "qb", "qa0", "qa1", "bx", "ap", "sx", "sent", "sadd", "qs",
-               "yd", "st"]
+SEMAPHORES = (["lb", "la0", "la1", "one", "ramp", "col", "zsel", "qe", "qb", "qa0", "qa1", "bx", "ap", "sx", "sent",
+               "sadd", "qs", "yd", "st"]
               + ["%s_%d" % (k, i) for k in ("p1", "p2", "p3", "p4", "p5", "r1", "r2", "r3", "r4", "a4") for i in range(4)])
 
 
@@ -48,20 +49,25 @@ def rank_program(g, core, T, topo):
         return RemoteDMATransfer(dst_ids=[DstId(rid=rid, pnc=pid)], dma_engine_mask=m, remote_sem=sem, src=in_, dst=out)
 
     g.sync.dma_start(T.b_in[:], T.b[:]).then_inc(S.lb, 16)
-    g.scalar.dma_start(T.a_in[:, 0:1024], T.a[:, 0:1024]).then_inc(S.la0, 16)
+    g.sync.dma_start(T.a_in[:, 0:1024], T.a[:, 0:1024]).then_inc(S.la0, 16)
     g.sync.dma_start(T.a_in[:, 1024:2048], T.a[:, 1024:2048]).then_inc(S.la1, 16)
 
     v = g.vector
-    v.memset(T.z[:], 1.0).then_inc(S.zset, 1)
-    v.wait_ge(S.zsel, 1)
-    for i in range(4):
-        v.quantize_mx(tile(T.eq, i), tile(T.es, i), T.z[:, 3 - i:515 - i]).then_inc(S.qe, 1)
+    v.memset(T.one[:], 1.0).then_inc(S.one, 1)
+    v.wait_ge(S.one, 1)
+    v.tensor_tensor_scan(T.ramp[:], T.one[:], T.one[:], -1.0, AluOpType.mult, AluOpType.add).then_inc(S.ramp, 1)
     v.wait_ge(S.lb, 16)
     v.quantize_mx(T.bq[:], T.bs[:], T.b_in[:]).then_inc(S.qb, 1)
     for h in range(2):
         v.wait_ge(S["la%d" % h], 16)
         for i in (2 * h, 2 * h + 1):
             v.quantize_mx(tile(T.aq, i), tile(T.asc, i), T.a_in[:, 512 * i:512 * i + 512]).then_inc(S["qa%d" % h], 1)
+    v.wait_ge(S.ramp, 1)
+    v.wait_ge(S.col, 1)
+    v.tensor_scalar(T.z[:], T.ramp[:], T.col[:], None, AluOpType.is_equal).then_inc(S.zsel, 1)
+    v.wait_ge(S.zsel, 1)
+    for i in range(4):
+        v.quantize_mx(tile(T.eq, i), tile(T.es, i), T.z[:, 3 - i:515 - i]).then_inc(S.qe, 1)
     for i in range(4):
         v.wait_ge(S["r2_%d" % i], 1)
         v.wait_ge(S["r3_%d" % i], 1)
@@ -77,8 +83,7 @@ def rank_program(g, core, T, topo):
         v.wait_ge(S["p5_%d" % i], 1)
         v.tensor_tensor(T.yb[:, i:512:4], bank(i), T.acc[:, i:512:4], AluOpType.add).then_inc(S.yd, 1)
 
-    g.wait_ge(S.zset, 1)
-    g.affine_select(T.z[:], T.z[:], [[-1, 516]], AluOpType.is_equal, 0.0, 3, 4).then_inc(S.zsel, 1)
+    g.iota(T.col[:], [[0, 1]], 3, 4, allow_small_or_imprecise_dtypes=True).then_inc(S.col, 1)
     g.wait_ge(S.qb, 1)
     send(far, m_far, T.bxs[:], T.bs[:], S.bx)
     g.wait_ge(S.qa0, 2)

from concourse.bass import DstId, RemoteDMATransfer
from concourse.mybir import dt, AluOpType, ActivationFunctionType

BF, F32, MX, U8 = "bfloat16", "float32", "float8_e4m3fn_x4", "uint8"
SCRATCH = {
    "b_in": ("sbuf", [128, 512], BF), "a_in": ("sbuf", [128, 2048], BF),
    "bq": ("sbuf", [128, 128], MX), "bs": ("sbuf", [128, 128], U8),
    "aq": ("sbuf", [128, 512], MX), "asc": ("sbuf", [128, 512], U8),
    "bxq": ("sbuf", [128, 128], MX), "bxs": ("sbuf", [128, 128], U8),
    "apq": ("sbuf", [128, 512], MX), "aps": ("sbuf", [128, 512], U8),
    "one": ("sbuf", [128, 516], BF), "ramp": ("sbuf", [128, 516], F32), "col": ("sbuf", [128, 1], F32),
    "z": ("sbuf", [128, 516], BF),
    "eq": ("sbuf", [128, 512], MX), "es": ("sbuf", [128, 512], U8),
    "s": ("sbuf", [128, 512], BF), "sq": ("sbuf", [128, 128], MX), "ss": ("sbuf", [128, 128], U8),
    "sxq": ("sbuf", [128, 128], MX), "sxs": ("sbuf", [128, 128], U8),
    "accs": ("sbuf", [128, 512], F32), "tmp3": ("sbuf", [128, 512], F32),
    "acc": ("sbuf", [128, 512], F32), "tmp4": ("sbuf", [128, 512], F32), "yb": ("sbuf", [128, 512], F32),
    "ps": ("psum", [128, 4096], F32),
}
SEMAPHORES = (["lb", "la0", "la1", "one", "ramp", "col", "zsel", "qe", "qb", "qa0", "qa1", "bx", "ap", "sx", "sent",
               "sadd", "qs", "yd", "st"]
              + ["%s_%d" % (k, i) for k in ("p1", "p2", "p3", "p4", "p5", "r1", "r2", "r3", "r4", "a4") for i in range(4)])


def rank_program(g, core, T, topo):
    rank = T.rank_of(core)
    if rank is None:
        return
    partner = [c for c in T.cores if c != core and topo.chip(c) == topo.chip(core)][0]
    far = [c for c in T.cores if topo.chip(c) != topo.chip(core) and topo.die(c) == topo.die(core)][0]
    m_near, m_far = topo.mask(core, partner), topo.mask(core, far)
    m_rest = m_near & ~m_far
    count = lambda m: bin(m).count("1")
    S = T.sem
    relu = ActivationFunctionType.Relu
    bank = lambda k: T.ps[:, 512 * k:512 * k + 128]
    tile = lambda t, i: t[:, 128 * i:128 * i + 128]
    codes = lambda v: v.bitcast(dt.uint8)
    sent = [0]

    def send(dst, m, out, in_, sem):
        rid, pid, _ = topo.addr(dst)
        g.remote_dma(out, in_, sem, S.sent, pid, rid, m)
        sent[0] += count(m)

    def part(dst, m, out, in_, sem):
        rid, pid, _ = topo.addr(dst)
        sent[0] += count(m)
        return RemoteDMATransfer(dst_ids=[DstId(rid=rid, pnc=pid)], dma_engine_mask=m, remote_sem=sem, src=in_, dst=out)

    g.sync.dma_start(T.b_in[:], T.b[:]).then_inc(S.lb, 16)
    g.sync.dma_start(T.a_in[:, 0:1024], T.a[:, 0:1024]).then_inc(S.la0, 16)
    g.sync.dma_start(T.a_in[:, 1024:2048], T.a[:, 1024:2048]).then_inc(S.la1, 16)

    v = g.vector
    v.memset(T.one[:], 1.0).then_inc(S.one, 1)
    v.wait_ge(S.one, 1)
    v.tensor_tensor_scan(T.ramp[:], T.one[:], T.one[:], -1.0, AluOpType.mult, AluOpType.add).then_inc(S.ramp, 1)
    v.wait_ge(S.lb, 16)
    v.quantize_mx(T.bq[:], T.bs[:], T.b_in[:]).then_inc(S.qb, 1)
    for h in range(2):
        v.wait_ge(S["la%d" % h], 16)
        for i in (2 * h, 2 * h + 1):
            v.quantize_mx(tile(T.aq, i), tile(T.asc, i), T.a_in[:, 512 * i:512 * i + 512]).then_inc(S["qa%d" % h], 1)
    v.wait_ge(S.ramp, 1)
    v.wait_ge(S.col, 1)
    v.tensor_scalar(T.z[:], T.ramp[:], T.col[:], None, AluOpType.is_equal).then_inc(S.zsel, 1)
    v.wait_ge(S.zsel, 1)
    for i in range(4):
        v.quantize_mx(tile(T.eq, i), tile(T.es, i), T.z[:, 3 - i:515 - i]).then_inc(S.qe, 1)
    for i in range(4):
        v.wait_ge(S["r2_%d" % i], 1)
        v.wait_ge(S["r3_%d" % i], 1)
        v.tensor_tensor(T.s[:, i:512:4], tile(T.tmp3, i), tile(T.accs, i), AluOpType.add).then_inc(S.sadd, 1)
    v.wait_ge(S.sadd, 4)
    v.quantize_mx(T.sq[:], T.ss[:], T.s[:]).then_inc(S.qs, 1)
    for i in range(4):
        v.wait_ge(S["r1_%d" % i], 1)
        v.wait_ge(S["r4_%d" % i], 1)
        v.tensor_tensor(T.acc[:, i:512:4], T.acc[:, i:512:4], tile(T.tmp4, i), AluOpType.add).then_inc(S["a4_%d" % i], 1)
    for i in range(4):
        v.wait_ge(S["a4_%d" % i], 1)
        v.wait_ge(S["p5_%d" % i], 1)
        v.tensor_tensor(T.yb[:, i:512:4], bank(i), T.acc[:, i:512:4], AluOpType.add).then_inc(S.yd, 1)

    g.iota(T.col[:], [[0, 1]], 3, 4, allow_small_or_imprecise_dtypes=True).then_inc(S.col, 1)
    g.wait_ge(S.qb, 1)
    send(far, m_far, T.bxs[:], T.bs[:], S.bx)
    g.wait_ge(S.qa0, 2)
    g.wait_ge(S.qa1, 2)
    g.remote_dma_fused([part(far, m_far, codes(T.bxq[:]), codes(T.bq[:]), S.bx),
                        part(partner, m_rest, T.aps[:], T.asc[:], S.ap)], local_sem=S.sent)
    send(partner, m_near, codes(T.apq[:]), codes(T.aq[:]), S.ap)
    g.wait_ge(S.qs, 1)
    send(far, m_far, codes(T.sxq[:]), codes(T.sq[:]), S.sx)
    send(far, m_far, T.sxs[:], T.ss[:], S.sx)
    g.wait_ge(S.sent, sent[0])

    t = g.tensor

    def mm(k, w, ws, i, x, xs, sem):
        t.matmul_mx(bank(k), tile(w, i), tile(ws, i), x[:], xs[:], True, True).then_inc(S["%s_%d" % (sem, i)], 1)

    t.wait_ge(S.qb, 1)
    for i in range(4):
        if i % 2 == 0:
            t.wait_ge(S["qa%d" % (i // 2)], 2)
        mm(i, T.aq, T.asc, i, T.bq, T.bs, "p1")
    t.wait_ge(S.bx, 2 * count(m_far))
    for i in range(4):
        mm(4 + i, T.aq, T.asc, i, T.bxq, T.bxs, "p2")
    t.wait_ge(S.ap, count(m_rest) + count(m_near))
    for i in range(4):
        t.wait_ge(S["r1_%d" % i], 1)
        mm(i, T.apq, T.aps, i, T.bxq, T.bxs, "p3")
    for i in range(4):
        t.wait_ge(S["r2_%d" % i], 1)
        mm(4 + i, T.apq, T.aps, i, T.bq, T.bs, "p4")
    t.wait_ge(S.qe, 4)
    t.wait_ge(S.sx, 2 * count(m_far))
    for i in range(4):
        t.wait_ge(S["r3_%d" % i], 1)
        mm(i, T.eq, T.es, i, T.sxq, T.sxs, "p5")

    a = g.scalar
    for k, dst in ((1, lambda i: T.acc[:, i:512:4]), (2, lambda i: tile(T.accs, i)),
                   (3, lambda i: tile(T.tmp3, i)), (4, lambda i: tile(T.tmp4, i))):
        for i in range(4):
            a.wait_ge(S["p%d_%d" % (k, i)], 1)
            a.activation(dst(i), bank(i if k % 2 else 4 + i), relu).then_inc(S["r%d_%d" % (k, i)], 1)

    g.sync.wait_ge(S.yd, 4)
    g.sync.dma_start(T.y[:], T.yb[:]).then_inc(S.st, 16)
    g.sync.wait_ge(S.st, 16)
